import numpy as np
import ml_dtypes


def mxq(x, axis, fmt="e4m3"):
    dtype, down = {"e4m3": (ml_dtypes.float8_e4m3fn, 7), "e5m2": (ml_dtypes.float8_e5m2, 14)}[fmt]
    v = np.moveaxis(np.asarray(x, np.float32).astype(ml_dtypes.bfloat16).astype(np.float64), axis, -1)
    blocks = v.reshape(v.shape[:-1] + (-1, 32))
    amax = np.abs(blocks).max(-1, keepdims=True)
    byte = np.maximum(np.where(amax > 0, np.frexp(amax)[1] - 1 + 127, 0) - down, 1)
    scale = np.exp2(byte - 127.0)
    codes = (blocks / scale).astype(np.float32).astype(dtype).astype(np.float64)
    return np.moveaxis((codes * scale).reshape(v.shape), -1, axis)


WIDE = False


def mx_kscale(k):
    if not WIDE:
        return np.ones(k)
    levels = np.array([10, -10, 5, -5, 0])
    if k % 512:
        return np.exp2(np.random.permutation(np.resize(levels, k // 32))).repeat(32)
    a = np.empty((k // 512, 16))
    for p in range(k // 512):
        a[p, :8] = np.random.permutation(np.resize(levels, 8))
        for g in range(8):
            far = levels[np.abs(levels - a[p, g]) >= 10]
            a[p, g + 8] = far[np.random.randint(len(far))]
    return np.exp2(a.ravel()).repeat(32)


BF16 = ml_dtypes.bfloat16


def bf(x):
    return np.asarray(x, np.float32).astype(BF16)


def f64(x):
    return np.asarray(x).astype(np.float64)


E2M1 = np.array([0.0, 0.5, 1.0, 1.5, 2.0, 3.0, 4.0, 6.0, -0.0, -0.5, -1.0, -1.5, -2.0, -3.0, -4.0, -6.0])


def pack_weight(w, fmt):
    k, n = w.shape
    w = f64(bf(w)).reshape(k // 32, 32, n)
    amax = np.abs(w).max(1)
    if fmt == "e4m3":
        byte = np.frexp(amax)[1] - 1 + 127 - 7
    else:
        mant, ex = np.frexp(amax / 6.0)
        byte = np.where(mant > 0.5, ex, ex - 1) + 127
    byte = np.clip(np.where(amax > 0, byte, 1), 1, 254)
    scaled = (w * np.exp2(127.0 - byte)[:, None, :]).reshape(k, n).astype(np.float32)
    by_word = np.ascontiguousarray(scaled.reshape(k // 512, 128, 4, n).transpose(0, 1, 3, 2))
    if fmt == "e4m3":
        words = by_word.astype(ml_dtypes.float8_e4m3fn).view(np.uint8)
    else:
        c = by_word.astype(ml_dtypes.float4_e2m1fn).view(np.uint8) & 0xF
        words = c[..., 0::2] | (c[..., 1::2] << 4)
    return np.ascontiguousarray(words), np.ascontiguousarray(byte.astype(np.uint8).reshape(k // 512, 16, n))


def unpack_weight(words, scales, fmt):
    g, p, n, _ = words.shape
    if fmt == "e4m3":
        vals = np.ascontiguousarray(words).view(ml_dtypes.float8_e4m3fn).astype(np.float64)
    else:
        nib = np.empty((g, p, n, 4), np.uint8)
        nib[..., 0::2] = words & 0xF
        nib[..., 1::2] = words >> 4
        vals = E2M1[nib]
    vals = vals * np.repeat(np.exp2(scales.astype(np.float64) - 127.0), 8, axis=1)[..., None]
    return vals.transpose(0, 1, 3, 2).reshape(g * 512, n)
def pack4(w):
    words, scales = pack_weight(w, "e2m1")
    return words.reshape(words.shape[0], 128, -1), scales


def unpack4(words, scales):
    return unpack_weight(words.reshape(words.shape[0], 128, -1, 2), scales, "e2m1")


def planes(Y):
    n, m = Y.shape
    b = f64(bf(Y)).reshape(n // 32, 32, m)
    amax = np.abs(b).max(1)
    byte = np.clip(np.where(amax > 0, np.frexp(amax)[1] - 1 + 127 - 7, 1), 1, 254)
    codes = (b * np.exp2(127.0 - byte)[:, None, :]).reshape(n, m).astype(np.float32).astype(ml_dtypes.float8_e4m3fn).view(np.uint8)
    words = codes.reshape(n // 512, 128, 4, m).transpose(0, 1, 3, 2)
    return np.ascontiguousarray(words), np.ascontiguousarray(byte.astype(np.uint8).reshape(n // 512, 16, m))


B, P, L, D, T = 8, 128, 1024, 1024, 16

def replica_bank():
    tau = np.arange(L)[:, None] * (1 + 0.1 * np.linspace(-1, 1, D))[None, :]
    freq, phase = 0.05 + 0.4 * np.random.rand(T), 2 * np.pi * np.random.rand(T)
    re = sum(np.cos(2 * np.pi * f * tau + h) for f, h in zip(freq, phase))
    im = sum(np.sin(2 * np.pi * f * tau + h) for f, h in zip(freq, phase))
    return np.concatenate([re, im], axis=1) * np.sqrt(2 / (T * L))

def setup_inputs():
    s, t = mx_kscale(L), mx_kscale(L)
    x = np.random.randn(B + 1, P, L) * s
    w0 = 0.9 * np.random.randn(L, L) / np.sqrt(L) / s[:, None]
    w1 = 0.6 * np.random.randn(L, L) / np.sqrt(L) / s[:, None]
    shade = np.exp(0.3 * np.random.randn(L)) * t
    r = replica_bank() / t[:, None]
    gain = np.exp(0.8 * np.random.randn(D))
    w1_words, w1_scales = pack4(w1)
    r_words, r_scales = pack_weight(r, "e4m3")
    return {"x": bf(x), "w0": bf(w0), "w1_words": w1_words, "w1_scales": w1_scales, "shade": bf(shade),
            "r_words": r_words, "r_scales": r_scales, "gain": bf(gain)}

def reference(x, w0, w1_words, w1_scales, shade, r_words, r_scales, gain):
    xq = mxq(f64(x), 2)
    w0q = mxq(f64(w0), 0)
    w1 = unpack4(w1_words, w1_scales)
    r = unpack_weight(r_words, r_scales, "e4m3")
    u = (xq[1:].reshape(B * P, L) @ w0q) + (xq[:-1].reshape(B * P, L) @ w1)
    z = np.tanh(u) * f64(shade)
    c = mxq(z, 1) @ r
    c_re, c_im = c[:, :D], c[:, D:]
    y = ((c_re * c_re + c_im * c_im) * f64(gain)).reshape(B, P, D)
    Y = y.reshape(B * P, D).T
    words, scales = planes(Y)
    return y, words, scales

@@ -1,0 +1,467 @@
+from contextlib import ExitStack
+
+import concourse.mybir as mybir
+from concourse.masks import make_identity
+
+F32 = mybir.dt.float32
+BF16 = mybir.dt.bfloat16
+I32 = mybir.dt.int32
+U32 = mybir.dt.uint32
+U8 = mybir.dt.uint8
+FP8X4 = mybir.dt.float8_e4m3fn_x4
+FP4X4 = mybir.dt.float4_e2m1fn_x4
+ACT = mybir.ActivationFunctionType
+ALU = mybir.AluOpType
+
+B, P, L, D = 8, 128, 1024, 1024
+HALF = 512
+BANKS = 8
+SCALAR_COLS = 192
+
+FLOPS = 2 * B * P * L * (2 * L + 2 * D)
+
+
+def tile_inverse_filter_doppler_bank_k6_kernel(
+    tc, x, w0, w1_words, w1_scales, shade, r_words, r_scales, gain, out_0, out_1, out_2
+):
+    nc = tc.nc
+    with ExitStack() as ctx:
+        keep = ctx.enter_context(tc.tile_pool(name="keep", bufs=1))
+        work = ctx.enter_context(tc.tile_pool(name="work", bufs=3))
+        psum = ctx.enter_context(tc.psum_pool(name="psum", bufs=1))
+        ctx.enter_context(tc.manual_schedule())
+
+        def kept(name, shape, dtype):
+            return keep.tile(shape, dtype, name=name, align_bytes=64)
+
+        def passing(name, shape, dtype, bufs=3):
+            return work.tile(shape, dtype, name=name, bufs=bufs, align_bytes=64)
+
+        free_banks = list(range(BANKS))
+        held = {}
+
+        def take_bank(key):
+            n = free_banks[0]
+            free_banks.remove(n)
+            held[key] = (n, psum.tile([P, HALF], F32, name="bank%d" % n))
+            return held[key][1]
+
+        def read_bank(key):
+            n, bank = held[key]
+            free_banks.append(n)
+            return bank
+
+        ident = kept("ident", [P, P], F32)
+        warm = kept("warm", [P, 1], F32)
+        x_raw = [kept("x_raw%d" % b, [P, L], BF16) for b in range(B + 1)]
+        x_codes = [kept("x_codes%d" % b, [P, 2 * P], U32) for b in range(B + 1)]
+        x_scales = [kept("x_scales%d" % b, [P, 2 * P], U8) for b in range(B + 1)]
+        chunks = [(h, g) for h in range(2) for g in range(2)]
+        w0_raw = {c: kept("w0_raw%d%d" % c, [P, 4, HALF], BF16) for c in chunks}
+        w0_grouped = {c: kept("w0_grouped%d%d" % c, [P, HALF, 4], BF16) for c in chunks}
+        w0_codes = {c: kept("w0_codes%d%d" % c, [P, HALF], U32) for c in chunks}
+        w0_scales = {c: kept("w0_scales%d%d" % c, [P, HALF], U8) for c in chunks}
+        w1_codes = kept("w1_codes", [P, 2, 2 * L], U8)
+        w1_plane = kept("w1_plane", [P, 2, L], U8)
+        r_codes = {c: kept("r_codes%d%d" % c, [P, 2, HALF], U32) for c in chunks}
+        r_plane = kept("r_plane", [P, 2 * D], U8)
+        shade_rows = kept("shade_rows", [P, 8], BF16)
+        gain_rows = kept("gain_rows", [P, 8], BF16)
+        shade_all = kept("shade_all", [P, L], BF16)
+        gain_all = kept("gain_all", [P, D], BF16)
+        y_codes = kept("y_codes", [P, 2, B * P], U32)
+        y_scales = kept("y_scales", [P, 2, B * P], U8)
+        live = {}
+
+        def load_x(b):
+            nc.sync.dma_start(out=x_raw[b][:], in_=x[b])
+
+        def load_w0(h, g):
+            rows = w0[HALF * g : HALF * (g + 1), HALF * h : HALF * (h + 1)]
+            nc.sync.dma_start(out=w0_raw[h, g][:], in_=rows.rearrange("(p j) n -> p j n", j=4))
+
+        def load_w1():
+            nc.sync.dma_start(out=w1_codes[:].bitcast(I32), in_=w1_words.rearrange("g p n -> p g n").bitcast(I32))
+            for q in range(4):
+                nc.sync.dma_start(
+                    out=w1_plane[32 * q : 32 * q + 4, :, :].bitcast(I32),
+                    in_=w1_scales[:, 4 * q : 4 * q + 4, :].rearrange("g r n -> r g n").bitcast(I32),
+                )
+
+        def load_r_scales():
+            for q in range(4):
+                nc.sync.dma_start(
+                    out=r_plane[32 * q : 32 * q + 8, :].bitcast(I32),
+                    in_=r_scales[:, 4 * q : 4 * q + 4, :].bitcast(I32),
+                )
+
+        def load_r(d, g):
+            words = r_words[g].rearrange("p n t -> p (n t)").bitcast(I32)
+            nc.sync.dma_start(
+                out=r_codes[d, g][:].bitcast(I32),
+                in_=words.rearrange("p (c d n) -> p c d n", c=2, d=2)[:, :, d, :],
+            )
+
+        def turn_x(b):
+            bank = take_bank(("x", b))
+            words = x_raw[b][:].bitcast(F32)
+            for g in range(2):
+                for u in range(2):
+                    j = 2 * g + u
+                    nc.tensor.transpose(
+                        bank[:, P * j : P * (j + 1)], words[:, 256 * g + u : 256 * (g + 1) : 2], ident[:]
+                    )
+
+        def turn(kind, b, halves=(0, 1)):
+            bank = take_bank((kind, b, halves))
+            words = live[kind + "_bf", b][:].bitcast(F32)
+            for g in halves:
+                for u in range(2):
+                    j = 2 * g + u
+                    nc.tensor.transpose(bank[:, P * j : P * (j + 1)], words[:, P * j : P * (j + 1)], ident[:])
+
+        def group_out(key, halves=(0, 1)):
+            bank = read_bank(key)
+            grouped = passing("grouped", [P, L], BF16, bufs=4)
+            lo, hi = 256 * halves[0], 256 * (halves[-1] + 1)
+            nc.scalar.copy(
+                out=grouped[:].bitcast(F32)[:, lo:hi].rearrange("p (g r u) -> p g r u", r=P, u=2),
+                in_=bank[:, lo:hi].rearrange("p (g u r) -> p g r u", u=2, r=P),
+            )
+            for g in halves:
+                live["grouped", key[0], key[1], g] = grouped
+
+        def spread(rows, key):
+            bank = take_bank(key)
+            words = rows[:].bitcast(F32)
+            for m in range(4):
+                nc.tensor.transpose(bank[:, P * m : P * (m + 1)], words[:, m : m + 1].to_broadcast([P, P]), ident[:])
+
+        def shade_out():
+            bank = read_bank("shade").rearrange("p (m n) -> p m n", m=4)
+            words = shade_all[:].bitcast(F32)
+            for g in range(2):
+                nc.scalar.copy(
+                    out=words[:, 256 * g : 256 * (g + 1)].rearrange("p (u a b) -> p u a b", u=2, b=2),
+                    in_=bank[:, :, 64 * g : 64 * (g + 1)].rearrange("p (b u) a -> p u a b", u=2),
+                )
+
+        def gain_out():
+            bank = read_bank("gain")
+            nc.scalar.copy(
+                out=gain_all[:].bitcast(F32).rearrange("p (n m) -> p n m", m=4),
+                in_=bank[:].rearrange("p (m n) -> p n m", m=4),
+            )
+
+        def group_w0(h, g):
+            for engine_copy, lo, hi in (
+                (nc.scalar.copy, 0, SCALAR_COLS),
+                (nc.vector.tensor_copy, SCALAR_COLS, HALF),
+            ):
+                engine_copy(
+                    out=w0_grouped[h, g][:, lo:hi, :].rearrange("p (c i) t -> p c t i", i=4),
+                    in_=w0_raw[h, g][:, :, lo:hi].rearrange("p t (c i) -> p c t i", i=4),
+                )
+
+        def quant_w0(h, g):
+            nc.vector.quantize_mx(
+                out=w0_codes[h, g][:].bitcast(FP8X4),
+                scales=w0_scales[h, g][:],
+                in_=w0_grouped[h, g][:].rearrange("p n t -> p (n t)"),
+            )
+
+        def quant_x(b):
+            grouped = live["grouped", "x", b, 1]
+            nc.vector.quantize_mx(out=x_codes[b][:].bitcast(FP8X4), scales=x_scales[b][:], in_=grouped[:])
+
+        def quant_z(b):
+            grouped = live["grouped", "z", b, 1]
+            z_codes = passing("z_codes", [P, 2 * P], U32)
+            z_scales = passing("z_scales", [P, 2 * P], U8)
+            nc.vector.quantize_mx(out=z_codes[:].bitcast(FP8X4), scales=z_scales[:], in_=grouped[:])
+            live["z_mx", b] = (z_codes, z_scales)
+
+        def quant_y(b, g):
+            grouped = live["grouped", "y", b, g]
+            cols = slice(P * b, P * (b + 1))
+            nc.vector.quantize_mx(
+                out=y_codes[:, g, cols].bitcast(FP8X4),
+                scales=y_scales[:, g, cols],
+                in_=grouped[:, HALF * g : HALF * (g + 1)],
+            )
+
+        def pass_u(b, h, kind, g, start=False, stop=False):
+            bank = take_bank(("u", b, h)) if start else held["u", b, h][1]
+            tok = slice(P * g, P * (g + 1))
+            if kind == "w0":
+                xb = b + 1
+                rhs, rhs_scale = w0_codes[h, g][:].bitcast(FP8X4), w0_scales[h, g][:]
+            else:
+                xb = b
+                rhs = w1_codes[:, g, 2 * HALF * h : 2 * HALF * (h + 1)].bitcast(FP4X4)
+                rhs_scale = w1_plane[:, g, HALF * h : HALF * (h + 1)]
+            nc.tensor.matmul_mx(
+                out=bank[:],
+                lhsT=x_codes[xb][:, tok].bitcast(FP8X4),
+                lhsT_scale=x_scales[xb][:, tok],
+                rhs=rhs,
+                rhs_scale=rhs_scale,
+                start=start,
+                stop=stop,
+            )
+
+        def pair_u(b, h, kind, start=False, stop=False):
+            pass_u(b, h, kind, 0, start=start)
+            pass_u(b, h, kind, 1, stop=stop)
+
+        def limit(b, h):
+            bank = read_bank(("u", b, h))
+            soft = passing("soft", [P, HALF], F32)
+            nc.scalar.activation(
+                out=soft[:].rearrange("p (u c e) -> p u c e", u=2, e=2),
+                in_=bank[:].rearrange("p (c u e) -> p u c e", u=2, e=2),
+                func=ACT.Tanh,
+            )
+            live["soft", b, h] = soft
+
+        def shade_z(b, h):
+            if h == 0:
+                live["z_bf", b] = passing("z_bf", [P, L], BF16, bufs=4)
+            cols = slice(HALF * h, HALF * (h + 1))
+            nc.vector.tensor_tensor(
+                out=live["z_bf", b][:, cols], in0=live["soft", b, h][:], in1=shade_all[:, cols], op=ALU.mult
+            )
+
+        def stage_u(b, h):
+            pair_u(b, h, "w1", start=True)
+            pair_u(b, h, "w0", stop=True)
+            limit(b, h)
+
+        def stage_c(b, d):
+            z_codes, z_scales = live["z_mx", b]
+            for c in range(2):
+                bank = take_bank(("c", b, d, c))
+                for g in range(2):
+                    tok = slice(P * g, P * (g + 1))
+                    nc.tensor.matmul_mx(
+                        out=bank[:],
+                        lhsT=z_codes[:, tok].bitcast(FP8X4),
+                        lhsT_scale=z_scales[:, tok],
+                        rhs=r_codes[d, g][:, c, :].bitcast(FP8X4),
+                        rhs_scale=r_plane[4 * g : P, D * c + HALF * d : D * c + HALF * (d + 1)],
+                        start=(g == 0),
+                        stop=(g == 1),
+                    )
+                square = passing("square%d" % c, [P, HALF], F32)
+                nc.scalar.activation(out=square[:], in_=read_bank(("c", b, d, c))[:], func=ACT.Square)
+                live["square", b, d, c] = square
+
+        def add_power(b, d):
+            power = passing("power", [P, HALF], F32)
+            nc.vector.tensor_tensor(
+                out=power[:],
+                in0=live["square", b, d, 0][:],
+                in1=live["square", b, d, 1][:],
+                op=ALU.add,
+            )
+            live["power", b, d] = power
+
+        def gain_y(b, d):
+            if d == 0:
+                live["y", b] = passing("y_f32", [P, D], F32)
+            cols = slice(HALF * d, HALF * (d + 1))
+            nc.vector.tensor_tensor(
+                out=live["y", b][:, cols], in0=live["power", b, d][:], in1=gain_all[:, cols], op=ALU.mult
+            )
+
+        def round_y(b, d):
+            if d == 0:
+                live["y_bf", b] = passing("y_bf", [P, D], BF16)
+            cols = slice(HALF * d, HALF * (d + 1))
+            nc.vector.tensor_copy(
+                out=live["y_bf", b][:, cols].rearrange("p (u c e) -> p u c e", u=2, e=2),
+                in_=live["y", b][:, cols].rearrange("p (c u e) -> p u c e", u=2, e=2),
+            )
+
+        def store_y(b, lo=0, hi=D):
+            nc.sync.dma_start(out=out_0[b][:, lo:hi], in_=live["y", b][:, lo:hi])
+
+        def store_codes(b, lo=0, hi=2):
+            cols = slice(P * b, P * (b + 1))
+            words = out_1.rearrange("g p m t -> p g (m t)").bitcast(I32)
+            nc.sync.dma_start(out=words[:, lo:hi, cols], in_=y_codes[:, lo:hi, cols].bitcast(I32))
+
+        def store_scales(lo, hi):
+            for q in range(4):
+                nc.sync.dma_start(
+                    out=out_2[:, 4 * q : 4 * q + 4, lo:hi].rearrange("g r m -> r g m").bitcast(I32),
+                    in_=y_scales[32 * q : 32 * q + 4, :, lo:hi].bitcast(I32),
+                )
+
+        nc.vector.memset(w1_plane[:].bitcast(I32), 0)
+        nc.vector.memset(r_plane[:].bitcast(I32), 0)
+        make_identity(nc, ident[:])
+        nc.scalar.activation(out=warm[:], in_=ident[:, 0:1], func=ACT.Tanh)
+        nc.gpsimd.dma_start(out=shade_rows[:], in_=shade.rearrange("(n m) -> n m", m=8))
+        nc.gpsimd.dma_start(out=gain_rows[:], in_=gain.rearrange("(n m) -> n m", m=8))
+
+        load_w0(0, 0)
+        load_x(1)
+        load_x(0)
+        load_w0(0, 1)
+        load_w1()
+        load_w0(1, 0)
+        load_x(2)
+        load_w0(1, 1)
+        load_x(3)
+        load_x(4)
+        load_r_scales()
+        for d, g in chunks:
+            load_r(d, g)
+        for b in range(5, B + 1):
+            load_x(b)
+
+        group_w0(0, 0)
+        turn_x(1)
+        turn_x(0)
+        spread(shade_rows, "shade")
+        quant_w0(0, 0)
+        group_out(("x", 1))
+        group_out(("x", 0))
+        quant_x(1)
+        group_w0(0, 1)
+        quant_x(0)
+        quant_w0(0, 1)
+        shade_out()
+        pair_u(0, 0, "w0", start=True)
+        pair_u(0, 0, "w1", stop=True)
+        pair_u(0, 1, "w1", start=True)
+        pair_u(1, 0, "w1", start=True)
+        pair_u(1, 1, "w1", start=True)
+        group_w0(1, 0)
+        turn_x(2)
+        turn_x(3)
+        group_out(("x", 2))
+        quant_w0(1, 0)
+        quant_x(2)
+        group_w0(1, 1)
+        limit(0, 0)
+        group_out(("x", 3))
+        quant_w0(1, 1)
+        pass_u(0, 1, "w0", 0)
+        pair_u(1, 0, "w0", stop=True)
+        pass_u(1, 1, "w0", 0)
+        pair_u(2, 0, "w1", start=True)
+        pass_u(0, 1, "w0", 1, stop=True)
+        pass_u(1, 1, "w0", 1, stop=True)
+        shade_z(0, 0)
+        quant_x(3)
+        limit(0, 1)
+        limit(1, 0)
+        limit(1, 1)
+        pair_u(2, 1, "w1", start=True)
+        pair_u(2, 0, "w0", stop=True)
+        pair_u(2, 1, "w0", stop=True)
+        shade_z(0, 1)
+        shade_z(1, 0)
+        shade_z(1, 1)
+
+        turn("z", 0)
+        turn_x(4)
+        spread(gain_rows, "gain")
+        limit(2, 0)
+        group_out(("z", 0, (0, 1)))
+        limit(2, 1)
+        group_out(("x", 4))
+        gain_out()
+        shade_z(2, 0)
+        quant_z(0)
+        shade_z(2, 1)
+        quant_x(4)
+        pair_u(3, 0, "w1", start=True)
+        pair_u(3, 1, "w1", start=True)
+        stage_c(0, 0)
+        stage_c(0, 1)
+        add_power(0, 0)
+
+        first_stage = {2: [(4, 0), (4, 1)], 3: [(5, 0), (5, 1)], 4: [(6, 0), (6, 1)], 5: [(7, 0)], 6: [(7, 1)]}
+        for k in range(1, B - 1):
+            with_y = k >= 2
+            with_x = k + 4 <= B
+            turn("z", k)
+            if with_y:
+                turn("y", k - 2)
+            if with_x:
+                turn_x(k + 4)
+            group_out(("z", k, (0, 1)))
+            if with_y:
+                group_out(("y", k - 2, (0, 1)))
+            if with_x:
+                group_out(("x", k + 4))
+            gain_y(k - 1, 0)
+            add_power(k - 1, 1)
+            quant_z(k)
+            round_y(k - 1, 0)
+            gain_y(k - 1, 1)
+            store_y(k - 1)
+            if with_y:
+                quant_y(k - 2, 0)
+            round_y(k - 1, 1)
+            if with_y:
+                quant_y(k - 2, 1)
+                store_codes(k - 2)
+            if with_x:
+                quant_x(k + 4)
+            if k == 1:
+                for h in range(2):
+                    pair_u(3, h, "w0", stop=True)
+                    limit(3, h)
+                    shade_z(3, h)
+            for b, h in first_stage.get(k, []):
+                stage_u(b, h)
+                shade_z(b, h)
+            stage_c(k, 0)
+            if k < B - 2:
+                stage_c(k, 1)
+            add_power(k, 0)
+
+        turn("y", 5)
+        turn("z", 7)
+        group_out(("y", 5, (0, 1)))
+        group_out(("z", 7, (0, 1)))
+        gain_y(6, 0)
+        quant_y(5, 0)
+        round_y(6, 0)
+        quant_y(5, 1)
+        quant_z(7)
+        store_codes(5)
+        store_scales(0, 6 * P)
+        stage_c(6, 1)
+        stage_c(7, 0)
+        stage_c(7, 1)
+        add_power(6, 1)
+        gain_y(6, 1)
+        store_y(6)
+        add_power(7, 0)
+        round_y(6, 1)
+        gain_y(7, 0)
+        store_y(7, 0, HALF)
+        add_power(7, 1)
+        round_y(7, 0)
+        gain_y(7, 1)
+        store_y(7, HALF, D)
+        turn("y", 6)
+        turn("y", 7, (0,))
+        group_out(("y", 6, (0, 1)))
+        group_out(("y", 7, (0,)), (0,))
+        quant_y(6, 0)
+        round_y(7, 1)
+        turn("y", 7, (1,))
+        group_out(("y", 7, (1,)), (1,))
+        quant_y(6, 1)
+        store_codes(6)
+        quant_y(7, 0)
+        store_codes(7, 0, 1)
+        quant_y(7, 1)
+        store_codes(7, 1, 2)
+        store_scales(6 * P, B * P)

@@ -73,6 +73,9 @@ def tile_inverse_filter_doppler_bank_k6_kernel(
         y_scales = kept("y_scales", [P, 2, B * P], U8)
         live = {}
 
+        def by_pairs(tile, lo, hi):
+            return tile[:].rearrange("p (u c e) -> p u c e", u=2, e=2)[:, :, lo // 4 : hi // 4, :]
+
         def load_x(b):
             nc.sync.dma_start(out=x_raw[b][:], in_=x[b])
 
@@ -82,6 +85,8 @@ def tile_inverse_filter_doppler_bank_k6_kernel(
 
         def load_w1():
             nc.sync.dma_start(out=w1_codes[:].bitcast(I32), in_=w1_words.rearrange("g p n -> p g n").bitcast(I32))
+
+        def load_w1_scales():
             for q in range(4):
                 nc.sync.dma_start(
                     out=w1_plane[32 * q : 32 * q + 4, :, :].bitcast(I32),
@@ -117,14 +122,14 @@ def tile_inverse_filter_doppler_bank_k6_kernel(
             words = live[kind + "_bf", b][:].bitcast(F32)
             for g in halves:
                 for u in range(2):
-                    j = 2 * g + u
-                    nc.tensor.transpose(bank[:, P * j : P * (j + 1)], words[:, P * j : P * (j + 1)], ident[:])
+                    j, i = 2 * g + u, 2 * u + g
+                    nc.tensor.transpose(bank[:, P * j : P * (j + 1)], words[:, P * i : P * (i + 1)], ident[:])
 
-        def group_out(key, halves=(0, 1)):
+        def group_out(key, copy, halves=(0, 1)):
             bank = read_bank(key)
-            grouped = passing("grouped", [P, L], BF16, bufs=4)
+            grouped = passing("grouped", [P, L], BF16, bufs=6)
             lo, hi = 256 * halves[0], 256 * (halves[-1] + 1)
-            nc.scalar.copy(
+            copy(
                 out=grouped[:].bitcast(F32)[:, lo:hi].rearrange("p (g r u) -> p g r u", r=P, u=2),
                 in_=bank[:, lo:hi].rearrange("p (g u r) -> p g r u", u=2, r=P),
             )
@@ -137,31 +142,33 @@ def tile_inverse_filter_doppler_bank_k6_kernel(
             for m in range(4):
                 nc.tensor.transpose(bank[:, P * m : P * (m + 1)], words[:, m : m + 1].to_broadcast([P, P]), ident[:])
 
-        def shade_out():
-            bank = read_bank("shade").rearrange("p (m n) -> p m n", m=4)
-            words = shade_all[:].bitcast(F32)
-            for g in range(2):
-                nc.scalar.copy(
-                    out=words[:, 256 * g : 256 * (g + 1)].rearrange("p (u a b) -> p u a b", u=2, b=2),
-                    in_=bank[:, :, 64 * g : 64 * (g + 1)].rearrange("p (b u) a -> p u a b", u=2),
-                )
+        def shade_out(copy):
+            bank = read_bank("shade")
+            copy(
+                out=shade_all[:].bitcast(F32).rearrange("p (u n b) -> p u n b", u=2, b=2),
+                in_=bank[:].rearrange("p (b u n) -> p u n b", u=2, b=2),
+            )
 
-        def gain_out():
+        def sort_x(b, copy):
+            pairs = passing("x_bf", [P, L], BF16, bufs=3)
+            copy(
+                out=pairs[:].bitcast(F32).rearrange("p (u c) -> p u c", u=2),
+                in_=x_raw[b][:].bitcast(F32).rearrange("p (c u) -> p u c", u=2),
+            )
+            live["x_bf", b] = pairs
+
+        def gain_out(copy):
             bank = read_bank("gain")
-            nc.scalar.copy(
+            copy(
                 out=gain_all[:].bitcast(F32).rearrange("p (n m) -> p n m", m=4),
                 in_=bank[:].rearrange("p (m n) -> p n m", m=4),
             )
 
-        def group_w0(h, g):
-            for engine_copy, lo, hi in (
-                (nc.scalar.copy, 0, SCALAR_COLS),
-                (nc.vector.tensor_copy, SCALAR_COLS, HALF),
-            ):
-                engine_copy(
-                    out=w0_grouped[h, g][:, lo:hi, :].rearrange("p (c i) t -> p c t i", i=4),
-                    in_=w0_raw[h, g][:, :, lo:hi].rearrange("p t (c i) -> p c t i", i=4),
-                )
+        def group_w0(h, g, lo, hi, copy):
+            copy(
+                out=w0_grouped[h, g][:, lo:hi, :].rearrange("p (c i) t -> p c t i", i=4),
+                in_=w0_raw[h, g][:, :, lo:hi].rearrange("p t (c i) -> p c t i", i=4),
+            )
 
         def quant_w0(h, g):
             nc.vector.quantize_mx(
@@ -174,12 +181,18 @@ def tile_inverse_filter_doppler_bank_k6_kernel(
             grouped = live["grouped", "x", b, 1]
             nc.vector.quantize_mx(out=x_codes[b][:].bitcast(FP8X4), scales=x_scales[b][:], in_=grouped[:])
 
-        def quant_z(b):
-            grouped = live["grouped", "z", b, 1]
-            z_codes = passing("z_codes", [P, 2 * P], U32)
-            z_scales = passing("z_scales", [P, 2 * P], U8)
-            nc.vector.quantize_mx(out=z_codes[:].bitcast(FP8X4), scales=z_scales[:], in_=grouped[:])
-            live["z_mx", b] = (z_codes, z_scales)
+        def quant_z(b, halves=(0, 1)):
+            if ("z_mx", b) not in live:
+                z_codes = passing("z_codes", [P, 2 * P], U32, bufs=3)
+                z_scales = passing("z_scales", [P, 2 * P], U8, bufs=3)
+                live["z_mx", b] = (z_codes, z_scales)
+            z_codes, z_scales = live["z_mx", b]
+            lo, hi = P * halves[0], P * (halves[-1] + 1)
+            nc.vector.quantize_mx(
+                out=z_codes[:, lo:hi].bitcast(FP8X4),
+                scales=z_scales[:, lo:hi],
+                in_=live["grouped", "z", b, halves[0]][:, 4 * lo : 4 * hi],
+            )
 
         def quant_y(b, g):
             grouped = live["grouped", "y", b, g]
@@ -216,7 +229,7 @@ def tile_inverse_filter_doppler_bank_k6_kernel(
 
         def limit(b, h):
             bank = read_bank(("u", b, h))
-            soft = passing("soft", [P, HALF], F32)
+            soft = passing("soft", [P, HALF], F32, bufs=4)
             nc.scalar.activation(
                 out=soft[:].rearrange("p (u c e) -> p u c e", u=2, e=2),
                 in_=bank[:].rearrange("p (c u e) -> p u c e", u=2, e=2),
@@ -225,11 +238,14 @@ def tile_inverse_filter_doppler_bank_k6_kernel(
             live["soft", b, h] = soft
 
         def shade_z(b, h):
-            if h == 0:
+            if ("z_bf", b) not in live:
                 live["z_bf", b] = passing("z_bf", [P, L], BF16, bufs=4)
-            cols = slice(HALF * h, HALF * (h + 1))
+            lo, hi = HALF * h, HALF * (h + 1)
             nc.vector.tensor_tensor(
-                out=live["z_bf", b][:, cols], in0=live["soft", b, h][:], in1=shade_all[:, cols], op=ALU.mult
+                out=by_pairs(live["z_bf", b], lo, hi),
+                in0=live["soft", b, h][:].rearrange("p (u c e) -> p u c e", u=2, e=2),
+                in1=by_pairs(shade_all, lo, hi),
+                op=ALU.mult,
             )
 
         def stage_u(b, h):
@@ -237,50 +253,68 @@ def tile_inverse_filter_doppler_bank_k6_kernel(
             pair_u(b, h, "w0", stop=True)
             limit(b, h)
 
-        def stage_c(b, d):
+        def pass_pair_c(out, b, c, lo, hi):
             z_codes, z_scales = live["z_mx", b]
+            d = lo // HALF
+            for g in range(2):
+                tok = slice(P * g, P * (g + 1))
+                nc.tensor.matmul_mx(
+                    out=out,
+                    lhsT=z_codes[:, tok].bitcast(FP8X4),
+                    lhsT_scale=z_scales[:, tok],
+                    rhs=r_codes[d, g][:, c, lo - HALF * d : hi - HALF * d].bitcast(FP8X4),
+                    rhs_scale=r_plane[4 * g : P, D * c + lo : D * c + hi],
+                    start=(g == 0),
+                    stop=(g == 1),
+                )
+
+        def correlate(b, d, c):
+            pass_pair_c(take_bank(("c", b, d, c))[:], b, c, HALF * d, HALF * (d + 1))
+
+        def squares_of(b):
+            if ("squares", b) not in live:
+                live["squares", b] = passing("squares", [P, 2, D], F32, bufs=3)
+            return live["squares", b]
+
+        def square(b, d, c):
+            nc.scalar.activation(
+                out=squares_of(b)[:, c, HALF * d : HALF * (d + 1)], in_=read_bank(("c", b, d, c))[:], func=ACT.Square
+            )
+
+        def correlate_narrow(b, lo, hi):
+            width = hi - lo
+            bank = take_bank(("c", b, lo))
             for c in range(2):
-                bank = take_bank(("c", b, d, c))
-                for g in range(2):
-                    tok = slice(P * g, P * (g + 1))
-                    nc.tensor.matmul_mx(
-                        out=bank[:],
-                        lhsT=z_codes[:, tok].bitcast(FP8X4),
-                        lhsT_scale=z_scales[:, tok],
-                        rhs=r_codes[d, g][:, c, :].bitcast(FP8X4),
-                        rhs_scale=r_plane[4 * g : P, D * c + HALF * d : D * c + HALF * (d + 1)],
-                        start=(g == 0),
-                        stop=(g == 1),
-                    )
-                square = passing("square%d" % c, [P, HALF], F32)
-                nc.scalar.activation(out=square[:], in_=read_bank(("c", b, d, c))[:], func=ACT.Square)
-                live["square", b, d, c] = square
+                pass_pair_c(bank[:, width * c : width * (c + 1)], b, c, lo, hi)
 
-        def add_power(b, d):
-            power = passing("power", [P, HALF], F32)
-            nc.vector.tensor_tensor(
-                out=power[:],
-                in0=live["square", b, d, 0][:],
-                in1=live["square", b, d, 1][:],
-                op=ALU.add,
-            )
-            live["power", b, d] = power
-
-        def gain_y(b, d):
-            if d == 0:
-                live["y", b] = passing("y_f32", [P, D], F32)
-            cols = slice(HALF * d, HALF * (d + 1))
-            nc.vector.tensor_tensor(
-                out=live["y", b][:, cols], in0=live["power", b, d][:], in1=gain_all[:, cols], op=ALU.mult
+        def square_narrow(b, lo, hi):
+            nc.scalar.activation(
+                out=squares_of(b)[:, :, lo:hi],
+                in_=read_bank(("c", b, lo))[:, 0 : 2 * (hi - lo)].rearrange("p (c n) -> p c n", c=2),
+                func=ACT.Square,
             )
 
-        def round_y(b, d):
-            if d == 0:
-                live["y_bf", b] = passing("y_bf", [P, D], BF16)
-            cols = slice(HALF * d, HALF * (d + 1))
-            nc.vector.tensor_copy(
-                out=live["y_bf", b][:, cols].rearrange("p (u c e) -> p u c e", u=2, e=2),
-                in_=live["y", b][:, cols].rearrange("p (c u e) -> p u c e", u=2, e=2),
+        def add_power(b, lo=0, hi=D):
+            if ("power", b) not in live:
+                live["power", b] = passing("power", [P, D], F32, bufs=3)
+            squares = live["squares", b]
+            nc.vector.tensor_tensor(
+                out=live["power", b][:, lo:hi], in0=squares[:, 0, lo:hi], in1=squares[:, 1, lo:hi], op=ALU.add
+            )
+
+        def gain_y(b, lo=0, hi=D):
+            if ("y", b) not in live:
+                live["y", b] = passing("y_f32", [P, D], F32, bufs=4)
+            nc.vector.tensor_tensor(
+                out=live["y", b][:, lo:hi], in0=live["power", b][:, lo:hi], in1=gain_all[:, lo:hi], op=ALU.mult
+            )
+
+        def round_y(b, lo, hi, copy):
+            if ("y_bf", b) not in live:
+                live["y_bf", b] = passing("y_bf", [P, D], BF16, bufs=4)
+            copy(
+                out=by_pairs(live["y_bf", b], lo, hi),
+                in_=live["y", b][:, lo:hi].rearrange("p (c u e) -> p u c e", u=2, e=2),
             )
 
         def store_y(b, lo=0, hi=D):
@@ -298,169 +332,337 @@ def tile_inverse_filter_doppler_bank_k6_kernel(
                     in_=y_scales[32 * q : 32 * q + 4, :, lo:hi].bitcast(I32),
                 )
 
+        nc.scalar.dma_start(out=shade_rows[:], in_=shade.rearrange("(n m) -> n m", m=8))
+        load_x(0)
+        load_x(1)
+        nc.scalar.dma_start(out=gain_rows[:], in_=gain.rearrange("(n m) -> n m", m=8))
+        load_x(2)
+        load_w1()
         nc.vector.memset(w1_plane[:].bitcast(I32), 0)
         nc.vector.memset(r_plane[:].bitcast(I32), 0)
+        load_w1_scales()
         make_identity(nc, ident[:])
-        nc.scalar.activation(out=warm[:], in_=ident[:, 0:1], func=ACT.Tanh)
-        nc.gpsimd.dma_start(out=shade_rows[:], in_=shade.rearrange("(n m) -> n m", m=8))
-        nc.gpsimd.dma_start(out=gain_rows[:], in_=gain.rearrange("(n m) -> n m", m=8))
-
-        load_w0(0, 0)
-        load_x(1)
-        load_x(0)
-        load_w0(0, 1)
-        load_w1()
-        load_w0(1, 0)
-        load_x(2)
-        load_w0(1, 1)
-        load_x(3)
-        load_x(4)
-        load_r_scales()
-        for d, g in chunks:
-            load_r(d, g)
-        for b in range(5, B + 1):
-            load_x(b)
-
-        group_w0(0, 0)
-        turn_x(1)
-        turn_x(0)
         spread(shade_rows, "shade")
-        quant_w0(0, 0)
-        group_out(("x", 1))
-        group_out(("x", 0))
-        quant_x(1)
-        group_w0(0, 1)
-        quant_x(0)
-        quant_w0(0, 1)
-        shade_out()
-        pair_u(0, 0, "w0", start=True)
-        pair_u(0, 0, "w1", stop=True)
-        pair_u(0, 1, "w1", start=True)
-        pair_u(1, 0, "w1", start=True)
-        pair_u(1, 1, "w1", start=True)
-        group_w0(1, 0)
-        turn_x(2)
-        turn_x(3)
-        group_out(("x", 2))
-        quant_w0(1, 0)
-        quant_x(2)
-        group_w0(1, 1)
-        limit(0, 0)
-        group_out(("x", 3))
-        quant_w0(1, 1)
-        pass_u(0, 1, "w0", 0)
-        pair_u(1, 0, "w0", stop=True)
-        pass_u(1, 1, "w0", 0)
-        pair_u(2, 0, "w1", start=True)
-        pass_u(0, 1, "w0", 1, stop=True)
-        pass_u(1, 1, "w0", 1, stop=True)
-        shade_z(0, 0)
-        quant_x(3)
-        limit(0, 1)
-        limit(1, 0)
-        limit(1, 1)
-        pair_u(2, 1, "w1", start=True)
-        pair_u(2, 0, "w0", stop=True)
-        pair_u(2, 1, "w0", stop=True)
-        shade_z(0, 1)
-        shade_z(1, 0)
-        shade_z(1, 1)
-
-        turn("z", 0)
-        turn_x(4)
+        turn_x(0)
+        turn_x(1)
+        nc.scalar.activation(out=warm[:], in_=ident[:, 0:1], func=ACT.Tanh)
+        load_w0(0, 0)
         spread(gain_rows, "gain")
-        limit(2, 0)
-        group_out(("z", 0, (0, 1)))
-        limit(2, 1)
-        group_out(("x", 4))
-        gain_out()
-        shade_z(2, 0)
-        quant_z(0)
-        shade_z(2, 1)
-        quant_x(4)
+        shade_out(nc.scalar.copy)
+        load_w0(0, 1)
+        load_x(3)
+        turn_x(2)
+        group_out(("x", 0), nc.vector.tensor_copy)
+        load_x(4)
+        load_w0(1, 0)
+        quant_x(0)
+        group_out(("x", 1), nc.vector.tensor_copy)
+        group_out(("x", 2), nc.scalar.copy)
+        load_w0(1, 1)
+        pass_u(0, 0, "w1", 0, start=True)
+        load_r(0, 0)
+        group_w0(0, 0, 0, 128, nc.scalar.copy)
+        load_x(5)
+        pass_u(0, 1, "w1", 0, start=True)
+        group_w0(0, 0, 128, 256, nc.scalar.copy)
+        load_x(6)
+        pass_u(0, 1, "w1", 1)
+        pass_u(0, 0, "w1", 1)
+        quant_x(1)
+        gain_out(nc.vector.tensor_copy)
+        group_w0(0, 0, 256, 384, nc.vector.tensor_copy)
+        pass_u(1, 0, "w1", 0, start=True)
+        pass_u(1, 0, "w1", 1)
+        quant_x(2)
+        group_w0(0, 0, 384, 512, nc.vector.tensor_copy)
+        pass_u(2, 0, "w1", 0, start=True)
+        pass_u(1, 1, "w1", 0, start=True)
+        group_w0(0, 1, 384, 512, nc.scalar.copy)
+        turn_x(3)
+        group_w0(0, 1, 128, 256, nc.scalar.copy)
+        group_w0(0, 1, 0, 128, nc.vector.tensor_copy)
+        group_w0(0, 1, 256, 384, nc.vector.tensor_copy)
+        turn_x(4)
+        load_r_scales()
+        quant_w0(0, 0)
+        pass_u(1, 1, "w1", 1)
+        group_out(("x", 3), nc.scalar.copy)
+        quant_w0(0, 1)
+        group_w0(1, 0, 128, 256, nc.scalar.copy)
+        pass_u(2, 1, "w1", 0, start=True)
+        group_w0(1, 0, 256, 384, nc.vector.tensor_copy)
+        quant_x(3)
+        pass_u(0, 0, "w0", 0)
+        pass_u(2, 1, "w1", 1)
+        group_out(("x", 4), nc.scalar.copy)
+        group_w0(1, 0, 384, 512, nc.vector.tensor_copy)
+        pass_u(2, 0, "w1", 1)
+        group_w0(1, 0, 0, 128, nc.scalar.copy)
+        group_w0(1, 1, 128, 256, nc.vector.tensor_copy)
+        load_r(0, 1)
+        pass_u(0, 0, "w0", 1, stop=True)
+        group_w0(1, 1, 0, 128, nc.vector.tensor_copy)
+        group_w0(1, 1, 384, 512, nc.scalar.copy)
+        pass_u(1, 0, "w0", 0)
+        pass_u(1, 0, "w0", 1, stop=True)
+        pass_u(2, 0, "w0", 0)
+        group_w0(1, 1, 256, 384, nc.vector.tensor_copy)
+        pass_u(2, 0, "w0", 1, stop=True)
+        quant_w0(1, 0)
+        load_r(1, 0)
+        quant_w0(1, 1)
+        sort_x(5, nc.vector.tensor_copy)
         pair_u(3, 0, "w1", start=True)
+        limit(0, 0)
+        limit(1, 0)
+        shade_z(0, 0)
+        sort_x(6, nc.scalar.copy)
         pair_u(3, 1, "w1", start=True)
-        stage_c(0, 0)
-        stage_c(0, 1)
-        add_power(0, 0)
-
-        first_stage = {2: [(4, 0), (4, 1)], 3: [(5, 0), (5, 1)], 4: [(6, 0), (6, 1)], 5: [(7, 0)], 6: [(7, 1)]}
-        for k in range(1, B - 1):
-            with_y = k >= 2
-            with_x = k + 4 <= B
-            turn("z", k)
-            if with_y:
-                turn("y", k - 2)
-            if with_x:
-                turn_x(k + 4)
-            group_out(("z", k, (0, 1)))
-            if with_y:
-                group_out(("y", k - 2, (0, 1)))
-            if with_x:
-                group_out(("x", k + 4))
-            gain_y(k - 1, 0)
-            add_power(k - 1, 1)
-            quant_z(k)
-            round_y(k - 1, 0)
-            gain_y(k - 1, 1)
-            store_y(k - 1)
-            if with_y:
-                quant_y(k - 2, 0)
-            round_y(k - 1, 1)
-            if with_y:
-                quant_y(k - 2, 1)
-                store_codes(k - 2)
-            if with_x:
-                quant_x(k + 4)
-            if k == 1:
-                for h in range(2):
-                    pair_u(3, h, "w0", stop=True)
-                    limit(3, h)
-                    shade_z(3, h)
-            for b, h in first_stage.get(k, []):
-                stage_u(b, h)
-                shade_z(b, h)
-            stage_c(k, 0)
-            if k < B - 2:
-                stage_c(k, 1)
-            add_power(k, 0)
-
-        turn("y", 5)
+        pass_u(0, 1, "w0", 0)
+        pass_u(0, 1, "w0", 1, stop=True)
+        pass_u(1, 1, "w0", 0)
+        limit(0, 1)
+        quant_x(4)
+        pass_u(1, 1, "w0", 1, stop=True)
+        pass_u(2, 1, "w0", 0)
+        pass_u(2, 1, "w0", 1, stop=True)
+        shade_z(1, 0)
+        limit(1, 1)
+        pair_u(3, 1, "w0", stop=True)
+        turn("x", 5)
+        shade_z(0, 1)
+        turn("x", 6)
+        turn("z", 0)
+        limit(2, 0)
+        shade_z(1, 1)
+        shade_z(2, 0)
+        limit(2, 1)
+        group_out(("x", 5, (0, 1)), nc.scalar.copy)
+        turn("z", 1)
+        pair_u(3, 0, "w0", stop=True)
+        load_r(1, 1)
+        group_out(("z", 0, (0, 1)), nc.vector.tensor_copy)
+        pair_u(4, 0, "w1", start=True)
+        quant_x(5)
+        pair_u(4, 0, "w0", stop=True)
+        group_out(("z", 1, (0, 1)), nc.scalar.copy)
+        quant_z(0)
+        correlate(0, 0, 0)
+        quant_z(1)
+        limit(3, 0)
+        limit(3, 1)
+        load_x(7)
+        correlate(0, 0, 1)
+        shade_z(3, 0)
+        shade_z(2, 1)
+        limit(4, 0)
+        group_out(("x", 6, (0, 1)), nc.vector.tensor_copy)
+        square(0, 0, 0)
+        correlate(0, 1, 0)
+        square(0, 0, 1)
+        square(0, 1, 0)
+        correlate(0, 1, 1)
+        square(0, 1, 1)
+        shade_z(4, 0)
+        sort_x(7, nc.vector.tensor_copy)
+        pair_u(4, 1, "w1", start=True)
+        shade_z(3, 1)
+        turn("z", 2)
+        turn("x", 7)
+        turn("z", 3)
+        quant_x(6)
+        group_out(("z", 2, (0, 1)), nc.scalar.copy)
+        correlate(1, 0, 0)
+        group_out(("x", 7, (0, 1)), nc.scalar.copy)
+        add_power(0)
+        pair_u(4, 1, "w0", stop=True)
+        correlate(1, 0, 1)
+        group_out(("z", 3, (0, 1)), nc.scalar.copy)
+        quant_z(2)
+        gain_y(0)
+        square(1, 0, 0)
+        correlate(1, 1, 0)
+        pair_u(5, 0, "w1", start=True)
+        correlate(1, 1, 1)
+        limit(4, 1)
+        pair_u(5, 0, "w0", stop=True)
+        load_x(8)
+        quant_x(7)
+        correlate(2, 0, 0)
+        correlate(2, 0, 1)
+        correlate(2, 1, 0)
+        square(1, 0, 1)
+        quant_z(3)
+        square(1, 1, 0)
+        square(1, 1, 1)
+        store_y(0)
+        limit(5, 0)
+        round_y(0, 0, D, nc.vector.tensor_copy)
+        shade_z(4, 1)
+        pair_u(5, 1, "w1", start=True)
+        sort_x(8, nc.vector.tensor_copy)
+        pair_u(5, 1, "w0", stop=True)
+        square(2, 0, 0)
+        square(2, 0, 1)
+        square(2, 1, 0)
+        correlate(2, 1, 1)
+        limit(5, 1)
+        add_power(1)
+        correlate(3, 0, 0)
+        shade_z(5, 0)
+        gain_y(1)
+        square(2, 1, 1)
+        turn("z", 4)
+        turn("y", 0)
+        turn("x", 8)
+        square(3, 0, 0)
+        group_out(("z", 4, (0, 1)), nc.scalar.copy)
+        shade_z(5, 1)
+        turn("z", 5)
+        group_out(("y", 0, (0, 1)), nc.scalar.copy)
+        round_y(1, 0, D, nc.vector.tensor_copy)
+        correlate(3, 0, 1)
+        correlate(3, 1, 0)
+        group_out(("z", 5, (0, 1)), nc.scalar.copy)
+        correlate(3, 1, 1)
+        add_power(2)
+        quant_z(4)
+        store_y(1)
+        square(3, 0, 1)
+        correlate(4, 0, 0)
+        square(3, 1, 0)
+        gain_y(2)
+        square(3, 1, 1)
+        quant_y(0, 0)
+        group_out(("x", 8, (0, 1)), nc.scalar.copy)
+        pair_u(6, 1, "w1", start=True)
+        pair_u(6, 1, "w0", stop=True)
+        correlate(4, 0, 1)
+        limit(6, 1)
+        quant_z(5)
+        round_y(2, 0, D, nc.vector.tensor_copy)
+        square(4, 0, 0)
+        store_y(2)
+        correlate(4, 1, 0)
+        add_power(3)
+        shade_z(6, 1)
+        square(4, 0, 1)
+        pair_u(6, 0, "w1", start=True)
+        gain_y(3)
+        square(4, 1, 0)
+        pair_u(6, 0, "w0", stop=True)
+        correlate(4, 1, 1)
+        quant_y(0, 1)
+        limit(6, 0)
+        square(4, 1, 1)
+        round_y(3, 0, D, nc.vector.tensor_copy)
+        correlate(5, 0, 0)
+        shade_z(6, 0)
+        square(5, 0, 0)
+        correlate(5, 0, 1)
+        turn("y", 1)
+        add_power(4)
+        square(5, 0, 1)
+        store_codes(0)
+        turn("y", 2)
+        group_out(("y", 1, (0, 1)), nc.scalar.copy)
+        turn("y", 3)
+        turn("z", 6)
+        pair_u(7, 0, "w1", start=True)
+        group_out(("y", 2, (0, 1)), nc.scalar.copy)
+        quant_x(8)
+        group_out(("y", 3, (0, 1)), nc.scalar.copy)
+        correlate(5, 1, 0)
+        gain_y(4)
+        pair_u(7, 0, "w0", stop=True)
+        quant_y(1, 0)
+        pair_u(7, 1, "w1", start=True)
+        group_out(("z", 6, (0, 1)), nc.scalar.copy)
+        store_y(3)
+        quant_y(1, 1)
+        round_y(4, 0, D, nc.vector.tensor_copy)
+        limit(7, 0)
+        pair_u(7, 1, "w0", stop=True)
+        quant_z(6)
+        shade_z(7, 0)
+        quant_y(2, 0)
+        correlate(5, 1, 1)
+        square(5, 1, 0)
+        correlate(6, 0, 0)
+        quant_y(2, 1)
+        quant_y(3, 0)
+        limit(7, 1)
+        square(5, 1, 1)
+        shade_z(7, 1)
+        turn("y", 4)
         turn("z", 7)
-        group_out(("y", 5, (0, 1)))
-        group_out(("z", 7, (0, 1)))
-        gain_y(6, 0)
-        quant_y(5, 0)
-        round_y(6, 0)
-        quant_y(5, 1)
+        correlate(6, 0, 1)
+        square(6, 0, 0)
+        correlate(6, 1, 0)
+        group_out(("y", 4, (0, 1)), nc.scalar.copy)
+        add_power(5)
+        quant_y(3, 1)
+        group_out(("z", 7, (0, 1)), nc.scalar.copy)
+        gain_y(5)
+        correlate(6, 1, 1)
+        square(6, 0, 1)
+        store_codes(1)
+        add_power(6, 0, HALF)
+        square(6, 1, 0)
         quant_z(7)
-        store_codes(5)
-        store_scales(0, 6 * P)
-        stage_c(6, 1)
-        stage_c(7, 0)
-        stage_c(7, 1)
-        add_power(6, 1)
-        gain_y(6, 1)
+        square(6, 1, 1)
+        correlate_narrow(7, 0, 256)
+        correlate_narrow(7, 256, 512)
+        store_y(4)
+        gain_y(6, 0, HALF)
+        round_y(5, 0, D, nc.scalar.copy)
+        turn("y", 5)
+        square_narrow(7, 0, 256)
+        square_narrow(7, 256, 512)
+        add_power(6, HALF, D)
+        quant_y(4, 0)
+        gain_y(6, HALF, D)
+        add_power(7, 0, 256)
+        store_codes(2)
+        quant_y(4, 1)
+        correlate_narrow(7, 512, 768)
+        gain_y(7, 0, 256)
+        store_codes(3)
+        add_power(7, 256, 512)
+        group_out(("y", 5, (0, 1)), nc.scalar.copy)
+        correlate_narrow(7, 768, 1024)
+        quant_y(5, 0)
+        quant_y(5, 1)
+        square_narrow(7, 512, 768)
+        round_y(6, 0, HALF, nc.vector.tensor_copy)
+        gain_y(7, 256, 512)
+        store_y(5)
+        square_narrow(7, 768, 1024)
+        add_power(7, 512, 768)
+        round_y(6, HALF, D, nc.scalar.copy)
+        add_power(7, 768, 1024)
+        round_y(7, 0, 256, nc.scalar.copy)
         store_y(6)
-        add_power(7, 0)
-        round_y(6, 1)
-        gain_y(7, 0)
-        store_y(7, 0, HALF)
-        add_power(7, 1)
-        round_y(7, 0)
-        gain_y(7, 1)
-        store_y(7, HALF, D)
+        store_codes(4)
         turn("y", 6)
-        turn("y", 7, (0,))
-        group_out(("y", 6, (0, 1)))
-        group_out(("y", 7, (0,)), (0,))
+        gain_y(7, 512, 768)
+        round_y(7, 256, 512, nc.scalar.copy)
+        group_out(("y", 6, (0, 1)), nc.scalar.copy)
+        gain_y(7, 768, 1024)
+        round_y(7, 512, 768, nc.vector.tensor_copy)
+        round_y(7, 768, 1024, nc.vector.tensor_copy)
         quant_y(6, 0)
-        round_y(7, 1)
-        turn("y", 7, (1,))
-        group_out(("y", 7, (1,)), (1,))
+        turn("y", 7, (0,))
+        store_scales(0, 6 * P)
+        group_out(("y", 7, (0,)), nc.scalar.copy, (0,))
+        store_codes(5)
         quant_y(6, 1)
+        turn("y", 7, (1,))
+        store_y(7, 0, HALF)
+        store_y(7, HALF, D)
         store_codes(6)
         quant_y(7, 0)
+        group_out(("y", 7, (1,)), nc.scalar.copy, (1,))
         store_codes(7, 0, 1)
         quant_y(7, 1)
         store_codes(7, 1, 2)

from contextlib import ExitStack

import concourse.mybir as mybir
from concourse.masks import make_identity

F32 = mybir.dt.float32
BF16 = mybir.dt.bfloat16
I32 = mybir.dt.int32
U32 = mybir.dt.uint32
U8 = mybir.dt.uint8
FP8X4 = mybir.dt.float8_e4m3fn_x4
FP4X4 = mybir.dt.float4_e2m1fn_x4
ACT = mybir.ActivationFunctionType
ALU = mybir.AluOpType

B, P, L, D = 8, 128, 1024, 1024
HALF = 512
BANKS = 8
SCALAR_COLS = 192

FLOPS = 2 * B * P * L * (2 * L + 2 * D)


def tile_inverse_filter_doppler_bank_k6_kernel(
    tc, x, w0, w1_words, w1_scales, shade, r_words, r_scales, gain, out_0, out_1, out_2
):
    nc = tc.nc
    with ExitStack() as ctx:
        keep = ctx.enter_context(tc.tile_pool(name="keep", bufs=1))
        work = ctx.enter_context(tc.tile_pool(name="work", bufs=3))
        psum = ctx.enter_context(tc.psum_pool(name="psum", bufs=1))
        ctx.enter_context(tc.manual_schedule())

        def kept(name, shape, dtype):
            return keep.tile(shape, dtype, name=name, align_bytes=64)

        def passing(name, shape, dtype, bufs=3):
            return work.tile(shape, dtype, name=name, bufs=bufs, align_bytes=64)

        free_banks = list(range(BANKS))
        held = {}

        def take_bank(key):
            n = free_banks[0]
            free_banks.remove(n)
            held[key] = (n, psum.tile([P, HALF], F32, name="bank%d" % n))
            return held[key][1]

        def read_bank(key):
            n, bank = held[key]
            free_banks.append(n)
            return bank

        ident = kept("ident", [P, P], F32)
        warm = kept("warm", [P, 1], F32)
        x_raw = [kept("x_raw%d" % b, [P, L], BF16) for b in range(B + 1)]
        x_codes = [kept("x_codes%d" % b, [P, 2 * P], U32) for b in range(B + 1)]
        x_scales = [kept("x_scales%d" % b, [P, 2 * P], U8) for b in range(B + 1)]
        chunks = [(h, g) for h in range(2) for g in range(2)]
        w0_raw = {c: kept("w0_raw%d%d" % c, [P, 4, HALF], BF16) for c in chunks}
        w0_grouped = {c: kept("w0_grouped%d%d" % c, [P, HALF, 4], BF16) for c in chunks}
        w0_codes = {c: kept("w0_codes%d%d" % c, [P, HALF], U32) for c in chunks}
        w0_scales = {c: kept("w0_scales%d%d" % c, [P, HALF], U8) for c in chunks}
        w1_codes = kept("w1_codes", [P, 2, 2 * L], U8)
        w1_plane = kept("w1_plane", [P, 2, L], U8)
        r_codes = {c: kept("r_codes%d%d" % c, [P, 2, HALF], U32) for c in chunks}
        r_plane = kept("r_plane", [P, 2 * D], U8)
        shade_rows = kept("shade_rows", [P, 8], BF16)
        gain_rows = kept("gain_rows", [P, 8], BF16)
        shade_all = kept("shade_all", [P, L], BF16)
        gain_all = kept("gain_all", [P, D], BF16)
        y_codes = kept("y_codes", [P, 2, B * P], U32)
        y_scales = kept("y_scales", [P, 2, B * P], U8)
        live = {}

        def by_pairs(tile, lo, hi):
            return tile[:].rearrange("p (u c e) -> p u c e", u=2, e=2)[:, :, lo // 4 : hi // 4, :]

        def load_x(b):
            nc.sync.dma_start(out=x_raw[b][:], in_=x[b])

        def load_w0(h, g):
            rows = w0[HALF * g : HALF * (g + 1), HALF * h : HALF * (h + 1)]
            nc.sync.dma_start(out=w0_raw[h, g][:], in_=rows.rearrange("(p j) n -> p j n", j=4))

        def load_w1():
            nc.sync.dma_start(out=w1_codes[:].bitcast(I32), in_=w1_words.rearrange("g p n -> p g n").bitcast(I32))

        def load_w1_scales():
            for q in range(4):
                nc.sync.dma_start(
                    out=w1_plane[32 * q : 32 * q + 4, :, :].bitcast(I32),
                    in_=w1_scales[:, 4 * q : 4 * q + 4, :].rearrange("g r n -> r g n").bitcast(I32),
                )

        def load_r_scales():
            for q in range(4):
                nc.sync.dma_start(
                    out=r_plane[32 * q : 32 * q + 8, :].bitcast(I32),
                    in_=r_scales[:, 4 * q : 4 * q + 4, :].bitcast(I32),
                )

        def load_r(d, g):
            words = r_words[g].rearrange("p n t -> p (n t)").bitcast(I32)
            nc.sync.dma_start(
                out=r_codes[d, g][:].bitcast(I32),
                in_=words.rearrange("p (c d n) -> p c d n", c=2, d=2)[:, :, d, :],
            )

        def turn_x(b):
            bank = take_bank(("x", b))
            words = x_raw[b][:].bitcast(F32)
            for g in range(2):
                for u in range(2):
                    j = 2 * g + u
                    nc.tensor.transpose(
                        bank[:, P * j : P * (j + 1)], words[:, 256 * g + u : 256 * (g + 1) : 2], ident[:]
                    )

        def turn(kind, b, halves=(0, 1)):
            bank = take_bank((kind, b, halves))
            words = live[kind + "_bf", b][:].bitcast(F32)
            for g in halves:
                for u in range(2):
                    j, i = 2 * g + u, 2 * u + g
                    nc.tensor.transpose(bank[:, P * j : P * (j + 1)], words[:, P * i : P * (i + 1)], ident[:])

        def group_out(key, copy, halves=(0, 1)):
            bank = read_bank(key)
            grouped = passing("grouped", [P, L], BF16, bufs=6)
            lo, hi = 256 * halves[0], 256 * (halves[-1] + 1)
            copy(
                out=grouped[:].bitcast(F32)[:, lo:hi].rearrange("p (g r u) -> p g r u", r=P, u=2),
                in_=bank[:, lo:hi].rearrange("p (g u r) -> p g r u", u=2, r=P),
            )
            for g in halves:
                live["grouped", key[0], key[1], g] = grouped

        def spread(rows, key):
            bank = take_bank(key)
            words = rows[:].bitcast(F32)
            for m in range(4):
                nc.tensor.transpose(bank[:, P * m : P * (m + 1)], words[:, m : m + 1].to_broadcast([P, P]), ident[:])

        def shade_out(copy):
            bank = read_bank("shade")
            copy(
                out=shade_all[:].bitcast(F32).rearrange("p (u n b) -> p u n b", u=2, b=2),
                in_=bank[:].rearrange("p (b u n) -> p u n b", u=2, b=2),
            )

        def sort_x(b, copy):
            pairs = passing("x_bf", [P, L], BF16, bufs=3)
            copy(
                out=pairs[:].bitcast(F32).rearrange("p (u c) -> p u c", u=2),
                in_=x_raw[b][:].bitcast(F32).rearrange("p (c u) -> p u c", u=2),
            )
            live["x_bf", b] = pairs

        def gain_out(copy):
            bank = read_bank("gain")
            copy(
                out=gain_all[:].bitcast(F32).rearrange("p (n m) -> p n m", m=4),
                in_=bank[:].rearrange("p (m n) -> p n m", m=4),
            )

        def group_w0(h, g, lo, hi, copy):
            copy(
                out=w0_grouped[h, g][:, lo:hi, :].rearrange("p (c i) t -> p c t i", i=4),
                in_=w0_raw[h, g][:, :, lo:hi].rearrange("p t (c i) -> p c t i", i=4),
            )

        def quant_w0(h, g):
            nc.vector.quantize_mx(
                out=w0_codes[h, g][:].bitcast(FP8X4),
                scales=w0_scales[h, g][:],
                in_=w0_grouped[h, g][:].rearrange("p n t -> p (n t)"),
            )

        def quant_x(b):
            grouped = live["grouped", "x", b, 1]
            nc.vector.quantize_mx(out=x_codes[b][:].bitcast(FP8X4), scales=x_scales[b][:], in_=grouped[:])

        def quant_z(b, halves=(0, 1)):
            if ("z_mx", b) not in live:
                z_codes = passing("z_codes", [P, 2 * P], U32, bufs=3)
                z_scales = passing("z_scales", [P, 2 * P], U8, bufs=3)
                live["z_mx", b] = (z_codes, z_scales)
            z_codes, z_scales = live["z_mx", b]
            lo, hi = P * halves[0], P * (halves[-1] + 1)
            nc.vector.quantize_mx(
                out=z_codes[:, lo:hi].bitcast(FP8X4),
                scales=z_scales[:, lo:hi],
                in_=live["grouped", "z", b, halves[0]][:, 4 * lo : 4 * hi],
            )

        def quant_y(b, g):
            grouped = live["grouped", "y", b, g]
            cols = slice(P * b, P * (b + 1))
            nc.vector.quantize_mx(
                out=y_codes[:, g, cols].bitcast(FP8X4),
                scales=y_scales[:, g, cols],
                in_=grouped[:, HALF * g : HALF * (g + 1)],
            )

        def pass_u(b, h, kind, g, start=False, stop=False):
            bank = take_bank(("u", b, h)) if start else held["u", b, h][1]
            tok = slice(P * g, P * (g + 1))
            if kind == "w0":
                xb = b + 1
                rhs, rhs_scale = w0_codes[h, g][:].bitcast(FP8X4), w0_scales[h, g][:]
            else:
                xb = b
                rhs = w1_codes[:, g, 2 * HALF * h : 2 * HALF * (h + 1)].bitcast(FP4X4)
                rhs_scale = w1_plane[:, g, HALF * h : HALF * (h + 1)]
            nc.tensor.matmul_mx(
                out=bank[:],
                lhsT=x_codes[xb][:, tok].bitcast(FP8X4),
                lhsT_scale=x_scales[xb][:, tok],
                rhs=rhs,
                rhs_scale=rhs_scale,
                start=start,
                stop=stop,
            )

        def pair_u(b, h, kind, start=False, stop=False):
            pass_u(b, h, kind, 0, start=start)
            pass_u(b, h, kind, 1, stop=stop)

        def limit(b, h):
            bank = read_bank(("u", b, h))
            soft = passing("soft", [P, HALF], F32, bufs=4)
            nc.scalar.activation(
                out=soft[:].rearrange("p (u c e) -> p u c e", u=2, e=2),
                in_=bank[:].rearrange("p (c u e) -> p u c e", u=2, e=2),
                func=ACT.Tanh,
            )
            live["soft", b, h] = soft

        def shade_z(b, h):
            if ("z_bf", b) not in live:
                live["z_bf", b] = passing("z_bf", [P, L], BF16, bufs=4)
            lo, hi = HALF * h, HALF * (h + 1)
            nc.vector.tensor_tensor(
                out=by_pairs(live["z_bf", b], lo, hi),
                in0=live["soft", b, h][:].rearrange("p (u c e) -> p u c e", u=2, e=2),
                in1=by_pairs(shade_all, lo, hi),
                op=ALU.mult,
            )

        def stage_u(b, h):
            pair_u(b, h, "w1", start=True)
            pair_u(b, h, "w0", stop=True)
            limit(b, h)

        def pass_pair_c(out, b, c, lo, hi):
            z_codes, z_scales = live["z_mx", b]
            d = lo // HALF
            for g in range(2):
                tok = slice(P * g, P * (g + 1))
                nc.tensor.matmul_mx(
                    out=out,
                    lhsT=z_codes[:, tok].bitcast(FP8X4),
                    lhsT_scale=z_scales[:, tok],
                    rhs=r_codes[d, g][:, c, lo - HALF * d : hi - HALF * d].bitcast(FP8X4),
                    rhs_scale=r_plane[4 * g : P, D * c + lo : D * c + hi],
                    start=(g == 0),
                    stop=(g == 1),
                )

        def correlate(b, d, c):
            pass_pair_c(take_bank(("c", b, d, c))[:], b, c, HALF * d, HALF * (d + 1))

        def squares_of(b):
            if ("squares", b) not in live:
                live["squares", b] = passing("squares", [P, 2, D], F32, bufs=3)
            return live["squares", b]

        def square(b, d, c):
            nc.scalar.activation(
                out=squares_of(b)[:, c, HALF * d : HALF * (d + 1)], in_=read_bank(("c", b, d, c))[:], func=ACT.Square
            )

        def correlate_narrow(b, lo, hi):
            width = hi - lo
            bank = take_bank(("c", b, lo))
            for c in range(2):
                pass_pair_c(bank[:, width * c : width * (c + 1)], b, c, lo, hi)

        def square_narrow(b, lo, hi):
            nc.scalar.activation(
                out=squares_of(b)[:, :, lo:hi],
                in_=read_bank(("c", b, lo))[:, 0 : 2 * (hi - lo)].rearrange("p (c n) -> p c n", c=2),
                func=ACT.Square,
            )

        def add_power(b, lo=0, hi=D):
            if ("power", b) not in live:
                live["power", b] = passing("power", [P, D], F32, bufs=3)
            squares = live["squares", b]
            nc.vector.tensor_tensor(
                out=live["power", b][:, lo:hi], in0=squares[:, 0, lo:hi], in1=squares[:, 1, lo:hi], op=ALU.add
            )

        def gain_y(b, lo=0, hi=D):
            if ("y", b) not in live:
                live["y", b] = passing("y_f32", [P, D], F32, bufs=4)
            nc.vector.tensor_tensor(
                out=live["y", b][:, lo:hi], in0=live["power", b][:, lo:hi], in1=gain_all[:, lo:hi], op=ALU.mult
            )

        def round_y(b, lo, hi, copy):
            if ("y_bf", b) not in live:
                live["y_bf", b] = passing("y_bf", [P, D], BF16, bufs=4)
            copy(
                out=by_pairs(live["y_bf", b], lo, hi),
                in_=live["y", b][:, lo:hi].rearrange("p (c u e) -> p u c e", u=2, e=2),
            )

        def store_y(b, lo=0, hi=D):
            nc.sync.dma_start(out=out_0[b][:, lo:hi], in_=live["y", b][:, lo:hi])

        def store_codes(b, lo=0, hi=2):
            cols = slice(P * b, P * (b + 1))
            words = out_1.rearrange("g p m t -> p g (m t)").bitcast(I32)
            nc.sync.dma_start(out=words[:, lo:hi, cols], in_=y_codes[:, lo:hi, cols].bitcast(I32))

        def store_scales(lo, hi):
            for q in range(4):
                nc.sync.dma_start(
                    out=out_2[:, 4 * q : 4 * q + 4, lo:hi].rearrange("g r m -> r g m").bitcast(I32),
                    in_=y_scales[32 * q : 32 * q + 4, :, lo:hi].bitcast(I32),
                )

        nc.scalar.dma_start(out=shade_rows[:], in_=shade.rearrange("(n m) -> n m", m=8))
        load_x(0)
        load_x(1)
        nc.scalar.dma_start(out=gain_rows[:], in_=gain.rearrange("(n m) -> n m", m=8))
        load_x(2)
        load_w1()
        nc.vector.memset(w1_plane[:].bitcast(I32), 0)
        nc.vector.memset(r_plane[:].bitcast(I32), 0)
        load_w1_scales()
        make_identity(nc, ident[:])
        spread(shade_rows, "shade")
        turn_x(0)
        turn_x(1)
        nc.scalar.activation(out=warm[:], in_=ident[:, 0:1], func=ACT.Tanh)
        load_w0(0, 0)
        spread(gain_rows, "gain")
        shade_out(nc.scalar.copy)
        load_w0(0, 1)
        load_x(3)
        turn_x(2)
        group_out(("x", 0), nc.vector.tensor_copy)
        load_x(4)
        load_w0(1, 0)
        quant_x(0)
        group_out(("x", 1), nc.vector.tensor_copy)
        group_out(("x", 2), nc.scalar.copy)
        load_w0(1, 1)
        pass_u(0, 0, "w1", 0, start=True)
        load_r(0, 0)
        group_w0(0, 0, 0, 128, nc.scalar.copy)
        load_x(5)
        pass_u(0, 1, "w1", 0, start=True)
        group_w0(0, 0, 128, 256, nc.scalar.copy)
        load_x(6)
        pass_u(0, 1, "w1", 1)
        pass_u(0, 0, "w1", 1)
        quant_x(1)
        gain_out(nc.vector.tensor_copy)
        group_w0(0, 0, 256, 384, nc.vector.tensor_copy)
        pass_u(1, 0, "w1", 0, start=True)
        pass_u(1, 0, "w1", 1)
        quant_x(2)
        group_w0(0, 0, 384, 512, nc.vector.tensor_copy)
        pass_u(2, 0, "w1", 0, start=True)
        pass_u(1, 1, "w1", 0, start=True)
        group_w0(0, 1, 384, 512, nc.scalar.copy)
        turn_x(3)
        group_w0(0, 1, 128, 256, nc.scalar.copy)
        group_w0(0, 1, 0, 128, nc.vector.tensor_copy)
        group_w0(0, 1, 256, 384, nc.vector.tensor_copy)
        turn_x(4)
        load_r_scales()
        quant_w0(0, 0)
        pass_u(1, 1, "w1", 1)
        group_out(("x", 3), nc.scalar.copy)
        quant_w0(0, 1)
        group_w0(1, 0, 128, 256, nc.scalar.copy)
        pass_u(2, 1, "w1", 0, start=True)
        group_w0(1, 0, 256, 384, nc.vector.tensor_copy)
        quant_x(3)
        pass_u(0, 0, "w0", 0)
        pass_u(2, 1, "w1", 1)
        group_out(("x", 4), nc.scalar.copy)
        group_w0(1, 0, 384, 512, nc.vector.tensor_copy)
        pass_u(2, 0, "w1", 1)
        group_w0(1, 0, 0, 128, nc.scalar.copy)
        group_w0(1, 1, 128, 256, nc.vector.tensor_copy)
        load_r(0, 1)
        pass_u(0, 0, "w0", 1, stop=True)
        group_w0(1, 1, 0, 128, nc.vector.tensor_copy)
        group_w0(1, 1, 384, 512, nc.scalar.copy)
        pass_u(1, 0, "w0", 0)
        pass_u(1, 0, "w0", 1, stop=True)
        pass_u(2, 0, "w0", 0)
        group_w0(1, 1, 256, 384, nc.vector.tensor_copy)
        pass_u(2, 0, "w0", 1, stop=True)
        quant_w0(1, 0)
        load_r(1, 0)
        quant_w0(1, 1)
        sort_x(5, nc.vector.tensor_copy)
        pair_u(3, 0, "w1", start=True)
        limit(0, 0)
        limit(1, 0)
        shade_z(0, 0)
        sort_x(6, nc.scalar.copy)
        pair_u(3, 1, "w1", start=True)
        pass_u(0, 1, "w0", 0)
        pass_u(0, 1, "w0", 1, stop=True)
        pass_u(1, 1, "w0", 0)
        limit(0, 1)
        quant_x(4)
        pass_u(1, 1, "w0", 1, stop=True)
        pass_u(2, 1, "w0", 0)
        pass_u(2, 1, "w0", 1, stop=True)
        shade_z(1, 0)
        limit(1, 1)
        pair_u(3, 1, "w0", stop=True)
        turn("x", 5)
        shade_z(0, 1)
        turn("x", 6)
        turn("z", 0)
        limit(2, 0)
        shade_z(1, 1)
        shade_z(2, 0)
        limit(2, 1)
        group_out(("x", 5, (0, 1)), nc.scalar.copy)
        turn("z", 1)
        pair_u(3, 0, "w0", stop=True)
        load_r(1, 1)
        group_out(("z", 0, (0, 1)), nc.vector.tensor_copy)
        pair_u(4, 0, "w1", start=True)
        quant_x(5)
        pair_u(4, 0, "w0", stop=True)
        group_out(("z", 1, (0, 1)), nc.scalar.copy)
        quant_z(0)
        correlate(0, 0, 0)
        quant_z(1)
        limit(3, 0)
        limit(3, 1)
        load_x(7)
        correlate(0, 0, 1)
        shade_z(3, 0)
        shade_z(2, 1)
        limit(4, 0)
        group_out(("x", 6, (0, 1)), nc.vector.tensor_copy)
        square(0, 0, 0)
        correlate(0, 1, 0)
        square(0, 0, 1)
        square(0, 1, 0)
        correlate(0, 1, 1)
        square(0, 1, 1)
        shade_z(4, 0)
        sort_x(7, nc.vector.tensor_copy)
        pair_u(4, 1, "w1", start=True)
        shade_z(3, 1)
        turn("z", 2)
        turn("x", 7)
        turn("z", 3)
        quant_x(6)
        group_out(("z", 2, (0, 1)), nc.scalar.copy)
        correlate(1, 0, 0)
        group_out(("x", 7, (0, 1)), nc.scalar.copy)
        add_power(0)
        pair_u(4, 1, "w0", stop=True)
        correlate(1, 0, 1)
        group_out(("z", 3, (0, 1)), nc.scalar.copy)
        quant_z(2)
        gain_y(0)
        square(1, 0, 0)
        correlate(1, 1, 0)
        pair_u(5, 0, "w1", start=True)
        correlate(1, 1, 1)
        limit(4, 1)
        pair_u(5, 0, "w0", stop=True)
        load_x(8)
        quant_x(7)
        correlate(2, 0, 0)
        correlate(2, 0, 1)
        correlate(2, 1, 0)
        square(1, 0, 1)
        quant_z(3)
        square(1, 1, 0)
        square(1, 1, 1)
        store_y(0)
        limit(5, 0)
        round_y(0, 0, D, nc.vector.tensor_copy)
        shade_z(4, 1)
        pair_u(5, 1, "w1", start=True)
        sort_x(8, nc.vector.tensor_copy)
        pair_u(5, 1, "w0", stop=True)
        square(2, 0, 0)
        square(2, 0, 1)
        square(2, 1, 0)
        correlate(2, 1, 1)
        limit(5, 1)
        add_power(1)
        correlate(3, 0, 0)
        shade_z(5, 0)
        gain_y(1)
        square(2, 1, 1)
        turn("z", 4)
        turn("y", 0)
        turn("x", 8)
        square(3, 0, 0)
        group_out(("z", 4, (0, 1)), nc.scalar.copy)
        shade_z(5, 1)
        turn("z", 5)
        group_out(("y", 0, (0, 1)), nc.scalar.copy)
        round_y(1, 0, D, nc.vector.tensor_copy)
        correlate(3, 0, 1)
        correlate(3, 1, 0)
        group_out(("z", 5, (0, 1)), nc.scalar.copy)
        correlate(3, 1, 1)
        add_power(2)
        quant_z(4)
        store_y(1)
        square(3, 0, 1)
        correlate(4, 0, 0)
        square(3, 1, 0)
        gain_y(2)
        square(3, 1, 1)
        quant_y(0, 0)
        group_out(("x", 8, (0, 1)), nc.scalar.copy)
        pair_u(6, 1, "w1", start=True)
        pair_u(6, 1, "w0", stop=True)
        correlate(4, 0, 1)
        limit(6, 1)
        quant_z(5)
        round_y(2, 0, D, nc.vector.tensor_copy)
        square(4, 0, 0)
        store_y(2)
        correlate(4, 1, 0)
        add_power(3)
        shade_z(6, 1)
        square(4, 0, 1)
        pair_u(6, 0, "w1", start=True)
        gain_y(3)
        square(4, 1, 0)
        pair_u(6, 0, "w0", stop=True)
        correlate(4, 1, 1)
        quant_y(0, 1)
        limit(6, 0)
        square(4, 1, 1)
        round_y(3, 0, D, nc.vector.tensor_copy)
        correlate(5, 0, 0)
        shade_z(6, 0)
        square(5, 0, 0)
        correlate(5, 0, 1)
        turn("y", 1)
        add_power(4)
        square(5, 0, 1)
        store_codes(0)
        turn("y", 2)
        group_out(("y", 1, (0, 1)), nc.scalar.copy)
        turn("y", 3)
        turn("z", 6)
        pair_u(7, 0, "w1", start=True)
        group_out(("y", 2, (0, 1)), nc.scalar.copy)
        quant_x(8)
        group_out(("y", 3, (0, 1)), nc.scalar.copy)
        correlate(5, 1, 0)
        gain_y(4)
        pair_u(7, 0, "w0", stop=True)
        quant_y(1, 0)
        pair_u(7, 1, "w1", start=True)
        group_out(("z", 6, (0, 1)), nc.scalar.copy)
        store_y(3)
        quant_y(1, 1)
        round_y(4, 0, D, nc.vector.tensor_copy)
        limit(7, 0)
        pair_u(7, 1, "w0", stop=True)
        quant_z(6)
        shade_z(7, 0)
        quant_y(2, 0)
        correlate(5, 1, 1)
        square(5, 1, 0)
        correlate(6, 0, 0)
        quant_y(2, 1)
        quant_y(3, 0)
        limit(7, 1)
        square(5, 1, 1)
        shade_z(7, 1)
        turn("y", 4)
        turn("z", 7)
        correlate(6, 0, 1)
        square(6, 0, 0)
        correlate(6, 1, 0)
        group_out(("y", 4, (0, 1)), nc.scalar.copy)
        add_power(5)
        quant_y(3, 1)
        group_out(("z", 7, (0, 1)), nc.scalar.copy)
        gain_y(5)
        correlate(6, 1, 1)
        square(6, 0, 1)
        store_codes(1)
        add_power(6, 0, HALF)
        square(6, 1, 0)
        quant_z(7)
        square(6, 1, 1)
        correlate_narrow(7, 0, 256)
        correlate_narrow(7, 256, 512)
        store_y(4)
        gain_y(6, 0, HALF)
        round_y(5, 0, D, nc.scalar.copy)
        turn("y", 5)
        square_narrow(7, 0, 256)
        square_narrow(7, 256, 512)
        add_power(6, HALF, D)
        quant_y(4, 0)
        gain_y(6, HALF, D)
        add_power(7, 0, 256)
        store_codes(2)
        quant_y(4, 1)
        correlate_narrow(7, 512, 768)
        gain_y(7, 0, 256)
        store_codes(3)
        add_power(7, 256, 512)
        group_out(("y", 5, (0, 1)), nc.scalar.copy)
        correlate_narrow(7, 768, 1024)
        quant_y(5, 0)
        quant_y(5, 1)
        square_narrow(7, 512, 768)
        round_y(6, 0, HALF, nc.vector.tensor_copy)
        gain_y(7, 256, 512)
        store_y(5)
        square_narrow(7, 768, 1024)
        add_power(7, 512, 768)
        round_y(6, HALF, D, nc.scalar.copy)
        add_power(7, 768, 1024)
        round_y(7, 0, 256, nc.scalar.copy)
        store_y(6)
        store_codes(4)
        turn("y", 6)
        gain_y(7, 512, 768)
        round_y(7, 256, 512, nc.scalar.copy)
        group_out(("y", 6, (0, 1)), nc.scalar.copy)
        gain_y(7, 768, 1024)
        round_y(7, 512, 768, nc.vector.tensor_copy)
        round_y(7, 768, 1024, nc.vector.tensor_copy)
        quant_y(6, 0)
        turn("y", 7, (0,))
        store_scales(0, 6 * P)
        group_out(("y", 7, (0,)), nc.scalar.copy, (0,))
        store_codes(5)
        quant_y(6, 1)
        turn("y", 7, (1,))
        store_y(7, 0, HALF)
        store_y(7, HALF, D)
        store_codes(6)
        quant_y(7, 0)
        group_out(("y", 7, (1,)), nc.scalar.copy, (1,))
        store_codes(7, 0, 1)
        quant_y(7, 1)
        store_codes(7, 1, 2)
        store_scales(6 * P, B * P)
